import numpy as np
import ml_dtypes


def mxq(x, axis, fmt="e4m3"):
    dtype, down = {"e4m3": (ml_dtypes.float8_e4m3fn, 7), "e5m2": (ml_dtypes.float8_e5m2, 14)}[fmt]
    v = np.moveaxis(np.asarray(x, np.float32).astype(ml_dtypes.bfloat16).astype(np.float64), axis, -1)
    blocks = v.reshape(v.shape[:-1] + (-1, 32))
    amax = np.abs(blocks).max(-1, keepdims=True)
    byte = np.maximum(np.where(amax > 0, np.frexp(amax)[1] - 1 + 127, 0) - down, 1)
    scale = np.exp2(byte - 127.0)
    codes = (blocks / scale).astype(np.float32).astype(dtype).astype(np.float64)
    return np.moveaxis((codes * scale).reshape(v.shape), -1, axis)


WIDE = False


def mx_kscale(k, group=512):
    if not WIDE:
        return np.ones(k)
    levels = np.array([10, -10, 5, -5, 0])
    if group != 512:
        return np.exp2(np.random.permutation(np.resize(levels, k // group))).repeat(group)
    if k % 512:
        return np.exp2(np.random.permutation(np.resize(levels, k // 32))).repeat(32)
    a = np.empty((k // 512, 16))
    for p in range(k // 512):
        a[p, :8] = np.random.permutation(np.resize(levels, 8))
        for g in range(8):
            far = levels[np.abs(levels - a[p, g]) >= 10]
            a[p, g + 8] = far[np.random.randint(len(far))]
    return np.exp2(a.ravel()).repeat(32)


def f64(x):
    return np.asarray(x).astype(np.float64)


def bf(x):
    return np.asarray(x, np.float32).astype(ml_dtypes.bfloat16)


def planes(Y):
    r, m = Y.shape
    b = f64(bf(Y)).reshape(r // 32, 32, m)
    amax = np.abs(b).max(1)
    byte = np.clip(np.where(amax > 0, np.frexp(amax)[1] - 1 + 127 - 7, 1), 1, 254)
    codes = (b * np.exp2(127.0 - byte)[:, None, :]).reshape(r, m).astype(np.float32).astype(ml_dtypes.float8_e4m3fn).view(np.uint8)
    words = codes.reshape(r // 512, 128, 4, m).transpose(0, 1, 3, 2)
    return np.ascontiguousarray(words), np.ascontiguousarray(byte.astype(np.uint8).reshape(r // 512, 16, m))


G, D, M, N = 2, 256, 256, 512


def setup_inputs():
    n = np.random.standard_normal
    s_d = mx_kscale(D, 0)
    return {
        "x": (n((G, D, N)) * s_d[:, None]).astype(np.float32),
        "w1": (n((G, D, M)) / np.sqrt(D) / s_d[:, None]).astype(np.float32),
        "w2": (n((G, D, M)) / np.sqrt(D) / s_d[:, None]).astype(np.float32),
        "sh": (np.random.uniform(0.1, 0.4, (G, M, 1))).astype(np.float32),
        "d0": (np.random.uniform(2.0, 6.0, (G, M, N))).astype(np.float32),
        "dx": (n((G, D, N)) * s_d[:, None]).astype(np.float32),
        "og": (np.random.uniform(0.5, 2.0, (G, M, 1))).astype(np.float32),
        "base": (0.3 * n((G, M, N))).astype(np.float32),
    }


def reference(x, w1, w2, sh, d0, dx, og, base):
    w1q = mxq(f64(w1), 1, "e4m3")
    xq = mxq(f64(x), 1, "e4m3")
    z1 = w1q.transpose(0, 2, 1) @ xq
    dxq = mxq(f64(dx), 1, "e4m3")
    tz1 = w1q.transpose(0, 2, 1) @ dxq
    w2q = mxq(f64(w2), 1, "e4m3")
    z2 = w2q.transpose(0, 2, 1) @ xq
    tz2 = w2q.transpose(0, 2, 1) @ dxq
    q1 = f64(d0) - z1 * 2.0
    xq1 = tz1 * 2.0 * (-1.0)
    xh = xq1 * f64(sh) * (-1.0) * np.exp(q1 * f64(sh) * (-1.0)) * z2 + tz2 * np.exp(q1 * f64(sh) * (-1.0))
    y = xh * f64(og) + f64(base)
    Y = y.reshape(G * M, N)
    words, scales = planes(Y)
    return Y, words, scales

@@ -1,0 +1,298 @@
+from contextlib import ExitStack
+
+import concourse.mybir as mybir
+
+G, D, M, N = 2, 256, 256, 512
+FLOPS = 4 * 2 * G * D * M * N
+
+F32 = mybir.dt.float32
+BF16 = mybir.dt.bfloat16
+I32 = mybir.dt.int32
+U32 = mybir.dt.uint32
+U8 = mybir.dt.uint8
+FP8X4 = mybir.dt.float8_e4m3fn_x4
+ALU = mybir.AluOpType
+EXP = mybir.ActivationFunctionType.Exp
+
+P = 128
+PACK = 4
+ROWS = D // PACK
+HALVES = M // P
+CHUNKS = 2
+W = N // CHUNKS
+SPLIT = 160
+
+
+def tile_rows_pl_tnkernrbf_kernel(tc, x, w1, w2, sh, d0, dx, og, base, out_0, out_1, out_2):
+    nc = tc.nc
+    with ExitStack() as ctx:
+        sb = ctx.enter_context(tc.tile_pool(name="sb", bufs=1))
+        ps = ctx.enter_context(tc.psum_pool(name="ps", bufs=1))
+        ctx.enter_context(tc.manual_schedule())
+
+        def tile(name, shape, dtype):
+            return sb.tile(shape, dtype, name=name, align_bytes=64)
+
+        def cols(c):
+            return slice(c * W, (c + 1) * W)
+
+        pairs = [(c, g) for c in range(CHUNKS) for g in range(G)]
+
+        w_raw = [tile("w_raw%d" % i, [P, PACK, M], F32) for i in range(2)]
+        w_bf = [tile("w_bf%d" % i, [P, M * PACK], BF16) for i in range(2)]
+        w_codes = [tile("w_codes%d" % i, [P, M], U32) for i in range(2)]
+        w_scales = [tile("w_scales%d" % i, [P, M], U8) for i in range(2)]
+        x_raw = [[tile("x_raw%d%d" % (c, i), [P, PACK, W], F32) for i in range(2)] for c in range(CHUNKS)]
+        x_bf = [[tile("x_bf%d%d" % (c, i), [P, W * PACK], BF16) for i in range(2)] for c in range(CHUNKS)]
+        x_codes = [tile("x_codes%d" % c, [P, 2 * W], U32) for c in range(CHUNKS)]
+        x_scales = [tile("x_scales%d" % c, [P, 2 * W], U8) for c in range(CHUNKS)]
+        sh_t = tile("sh_t", [P, G, HALVES], F32)
+        og_t = tile("og_t", [P, G, HALVES], F32)
+        k_t = tile("k_t", [P, G, HALVES], F32)
+
+        def per_pair(name):
+            return dict((p, tile("%s%d%d" % (name, p[0], p[1]), [P, HALVES, W], F32)) for p in pairs)
+
+        d0_t, base_t = per_pair("d0"), per_pair("base")
+        q_t, e_t, z2_t, b_t, c_t, f_t, y_t = [per_pair(s) for s in ("q", "e", "z2", "b", "c", "f", "y")]
+        yb_t = dict((p, tile("yb%d%d" % p, [P, W * HALVES], BF16)) for p in pairs)
+        hop_t = [tile("hop%d" % c, [P, 2, W], F32) for c in range(CHUNKS)]
+        yq_t = [tile("yq%d" % c, [P, W * PACK], BF16) for c in range(CHUNKS)]
+        y_codes = tile("y_codes", [P, N], U32)
+        y_scales = tile("y_scales", [P, N], U8)
+
+        def k_rows(t):
+            return t.rearrange("g (p j) n -> (g p) j n", j=PACK)
+
+        def feature_rows(t, p):
+            c, g = p
+            return t.rearrange("(q h) n -> q h n", h=HALVES)[:, :, cols(c)]
+
+        def load_x(c, i):
+            nc.sync.dma_start(out=x_raw[c][i][:], in_=k_rows((x, dx)[i])[:, :, cols(c)])
+
+        def load_d0(p):
+            nc.sync.dma_start(out=d0_t[p][:], in_=feature_rows(d0[p[1]], p))
+
+        def load_base(p):
+            nc.sync.dma_start(out=base_t[p][:], in_=feature_rows(base[p[1]], p))
+
+        nc.sync.dma_start(out=w_raw[0][:], in_=k_rows(w1))
+        nc.sync.dma_start(out=w_raw[1][:], in_=k_rows(w2))
+        nc.scalar.dma_start(out=sh_t[:], in_=sh.rearrange("g (q h) o -> q g (h o)", h=HALVES))
+        nc.scalar.dma_start(out=og_t[:], in_=og.rearrange("g (q h) o -> q g (h o)", h=HALVES))
+        load_x(0, 0)
+        load_x(0, 1)
+        load_d0(pairs[0])
+        load_base(pairs[0])
+        load_d0(pairs[1])
+        load_x(1, 0)
+        load_x(1, 1)
+        load_base(pairs[1])
+        for p in pairs[2:]:
+            load_d0(p)
+            load_base(p)
+
+        def round_w(i):
+            nc.vector.tensor_copy(
+                out=w_bf[i][:].rearrange("p (h q j) -> p q j h", h=HALVES, j=PACK),
+                in_=w_raw[i][:].rearrange("p j (q h) -> p q j h", h=HALVES),
+            )
+
+        def quant_w(i):
+            nc.vector.quantize_mx(out=w_codes[i][:].bitcast(FP8X4), scales=w_scales[i][:], in_=w_bf[i][:])
+
+        def round_x(copy, c, i, lo, hi):
+            copy(
+                out=x_bf[c][i][:, lo * PACK : hi * PACK].rearrange("p (a b j) -> p a j b", b=4, j=PACK),
+                in_=x_raw[c][i][:, :, lo:hi].rearrange("p j (a b) -> p a j b", b=4),
+            )
+
+        def quant_x(c, i):
+            nc.vector.quantize_mx(
+                out=x_codes[c][:, i * W : (i + 1) * W].bitcast(FP8X4),
+                scales=x_scales[c][:, i * W : (i + 1) * W],
+                in_=x_bf[c][i][:],
+            )
+
+        acc = {}
+
+        def matmul(c, g, h, i):
+            rows = slice(g * ROWS, (g + 1) * ROWS)
+            feats = slice(h * P, (h + 1) * P)
+            bank = ps.tile([P, 2 * W], F32, name="acc%d%d%d" % (g, h, i))
+            acc[(c, g, h, i)] = bank
+            nc.tensor.matmul_mx(
+                out=bank[:],
+                lhsT=w_codes[i][rows, feats].bitcast(FP8X4),
+                lhsT_scale=w_scales[i][rows, feats],
+                rhs=x_codes[c][rows, :].bitcast(FP8X4),
+                rhs_scale=x_scales[c][rows, :],
+                start=True,
+                stop=True,
+            )
+
+        def copy_z2(p, h):
+            nc.scalar.copy(out=z2_t[p][:, h, :], in_=acc[p + (h, 1)][:, 0:W])
+
+        def dist(p, h):
+            nc.vector.scalar_tensor_tensor(
+                out=q_t[p][:, h, :], in0=acc[p + (h, 0)][:, 0:W], scalar=2.0, in1=d0_t[p][:, h, :],
+                op0=ALU.mult, op1=ALU.subtract,
+            )
+
+        def expo(p, h):
+            nc.scalar.activation(out=e_t[p][:, h, :], in_=q_t[p][:, h, :], func=EXP, scale=sh_t[:, p[1], h : h + 1])
+
+        def prod(p, h):
+            nc.vector.scalar_tensor_tensor(
+                out=b_t[p][:, h, :], in0=acc[p + (h, 0)][:, W : 2 * W], scalar=k_t[:, p[1], h : h + 1],
+                in1=z2_t[p][:, h, :], op0=ALU.mult, op1=ALU.mult,
+            )
+
+        def plus(p, h):
+            nc.vector.scalar_tensor_tensor(
+                out=c_t[p][:, h, :], in0=acc[p + (h, 1)][:, W : 2 * W], scalar=og_t[:, p[1], h : h + 1],
+                in1=b_t[p][:, h, :], op0=ALU.mult, op1=ALU.add,
+            )
+
+        def weigh(p, lo=0, hi=W):
+            nc.vector.tensor_tensor(out=f_t[p][:, :, lo:hi], in0=c_t[p][:, :, lo:hi], in1=e_t[p][:, :, lo:hi], op=ALU.mult)
+
+        def finish(p):
+            nc.vector.tensor_tensor(out=y_t[p][:], in0=f_t[p][:], in1=base_t[p][:], op=ALU.add)
+
+        def finish_bf(p, lo, hi):
+            nc.vector.tensor_tensor(
+                out=yb_t[p][:, lo * HALVES : hi * HALVES].rearrange("q (n h) -> q n h", h=HALVES),
+                in0=f_t[p][:, :, lo:hi].rearrange("q h n -> q n h"),
+                in1=base_t[p][:, :, lo:hi].rearrange("q h n -> q n h"),
+                op=ALU.add,
+            )
+
+        def round_y(p):
+            nc.scalar.copy(
+                out=yb_t[p][:].rearrange("q (n h) -> q n h", h=HALVES), in_=y_t[p][:].rearrange("q h n -> q n h")
+            )
+
+        def store_y(p):
+            nc.sync.dma_start(out=feature_rows(out_0[p[1] * M : (p[1] + 1) * M, :], p), in_=y_t[p][:])
+
+        def hop(p):
+            c, g = p
+            nc.sync.dma_start(out=hop_t[c][g * ROWS : (g + 1) * ROWS, :, :], in_=yb_t[p][:].bitcast(F32))
+
+        def regroup(copy, c):
+            copy(
+                out=yq_t[c][:].bitcast(F32).rearrange("p (n r) -> p n r", r=2),
+                in_=hop_t[c][:].rearrange("p r n -> p n r"),
+            )
+
+        def quant_y(c):
+            nc.vector.quantize_mx(out=y_codes[:, cols(c)].bitcast(FP8X4), scales=y_scales[:, cols(c)], in_=yq_t[c][:])
+
+        def store_words(c):
+            nc.sync.dma_start(
+                out=out_1[0].rearrange("p n u -> p (n u)").bitcast(I32)[:, cols(c)],
+                in_=y_codes[:, cols(c)].bitcast(I32),
+            )
+
+        def store_scales(queue, quad):
+            queue.dma_start(
+                out=out_2[0, 4 * quad : 4 * quad + 4, :].bitcast(I32),
+                in_=y_scales[32 * quad : 32 * quad + 4, :].bitcast(I32),
+            )
+
+        p0, p1, p2, p3 = pairs
+
+        round_w(0)
+        quant_w(0)
+        round_w(1)
+        nc.vector.scalar_tensor_tensor(out=k_t[:], in0=sh_t[:], scalar=2.0, in1=og_t[:], op0=ALU.mult, op1=ALU.mult)
+        quant_w(1)
+        round_x(nc.vector.tensor_copy, 0, 0, 0, W)
+        quant_x(0, 0)
+        round_x(nc.vector.tensor_copy, 0, 1, 0, SPLIT)
+        round_x(nc.scalar.copy, 0, 1, SPLIT, W)
+        quant_x(0, 1)
+        for g, h, i in [(0, 0, 1), (0, 0, 0), (0, 1, 1), (1, 0, 1), (0, 1, 0), (1, 0, 0), (1, 1, 1), (1, 1, 0)]:
+            matmul(0, g, h, i)
+
+        copy_z2(p0, 0)
+        dist(p0, 0)
+        prod(p0, 0)
+        expo(p0, 0)
+        copy_z2(p0, 1)
+        plus(p0, 0)
+        dist(p0, 1)
+        prod(p0, 1)
+        round_x(nc.scalar.copy, 1, 0, 0, W // 2)
+        expo(p0, 1)
+        copy_z2(p1, 0)
+        dist(p1, 0)
+        plus(p0, 1)
+        round_x(nc.scalar.copy, 1, 0, W // 2, W)
+        copy_z2(p1, 1)
+        dist(p1, 1)
+        weigh(p0)
+        prod(p1, 0)
+        finish(p0)
+        store_y(p0)
+        round_x(nc.scalar.copy, 1, 1, 0, W // 2)
+        expo(p1, 0)
+        round_x(nc.scalar.copy, 1, 1, W // 2, W)
+        expo(p1, 1)
+        quant_x(1, 0)
+        prod(p1, 1)
+        plus(p1, 0)
+        quant_x(1, 1)
+        plus(p1, 1)
+        for g, h, i in [(0, 0, 1), (0, 0, 0), (0, 1, 1), (1, 0, 1), (0, 1, 0), (1, 0, 0), (1, 1, 1), (1, 1, 0)]:
+            matmul(1, g, h, i)
+        round_y(p0)
+        hop(p0)
+        weigh(p1)
+        copy_z2(p2, 0)
+        dist(p2, 0)
+        finish(p1)
+        store_y(p1)
+        expo(p2, 0)
+        copy_z2(p2, 1)
+        prod(p2, 0)
+        dist(p2, 1)
+        plus(p2, 0)
+        expo(p2, 1)
+        round_y(p1)
+        hop(p1)
+        prod(p2, 1)
+        copy_z2(p3, 0)
+        copy_z2(p3, 1)
+        dist(p3, 0)
+        plus(p2, 1)
+        dist(p3, 1)
+        expo(p3, 0)
+        expo(p3, 1)
+        weigh(p2)
+        prod(p3, 0)
+        finish(p2)
+        store_y(p2)
+        round_y(p2)
+        hop(p2)
+        regroup(nc.scalar.copy, 0)
+        prod(p3, 1)
+        plus(p3, 0)
+        plus(p3, 1)
+        quant_y(0)
+        store_words(0)
+        weigh(p3, 0, W // 2)
+        weigh(p3, W // 2, W)
+        finish_bf(p3, 0, W // 2)
+        finish_bf(p3, W // 2, W)
+        hop(p3)
+        finish(p3)
+        store_y(p3)
+        regroup(nc.vector.tensor_copy, 1)
+        quant_y(1)
+        store_words(1)
+        for quad in range(4):
+            store_scales((nc.scalar, nc.sync)[quad % 2], quad)

@@ -21,6 +21,7 @@ HALVES = M // P
 CHUNKS = 2
 W = N // CHUNKS
 SPLIT = 160
+NT = 128
 
 
 def tile_rows_pl_tnkernrbf_kernel(tc, x, w1, w2, sh, d0, dx, og, base, out_0, out_1, out_2):
@@ -44,8 +45,8 @@ def tile_rows_pl_tnkernrbf_kernel(tc, x, w1, w2, sh, d0, dx, og, base, out_0, ou
         w_scales = [tile("w_scales%d" % i, [P, M], U8) for i in range(2)]
         x_raw = [[tile("x_raw%d%d" % (c, i), [P, PACK, W], F32) for i in range(2)] for c in range(CHUNKS)]
         x_bf = [[tile("x_bf%d%d" % (c, i), [P, W * PACK], BF16) for i in range(2)] for c in range(CHUNKS)]
-        x_codes = [tile("x_codes%d" % c, [P, 2 * W], U32) for c in range(CHUNKS)]
-        x_scales = [tile("x_scales%d" % c, [P, 2 * W], U8) for c in range(CHUNKS)]
+        x_codes = [[tile("x_codes%d%d" % (c, i), [P, W], U32) for i in range(2)] for c in range(CHUNKS)]
+        x_scales = [[tile("x_scales%d%d" % (c, i), [P, W], U8) for i in range(2)] for c in range(CHUNKS)]
         sh_t = tile("sh_t", [P, G, HALVES], F32)
         og_t = tile("og_t", [P, G, HALVES], F32)
         k_t = tile("k_t", [P, G, HALVES], F32)
@@ -77,21 +78,22 @@ def tile_rows_pl_tnkernrbf_kernel(tc, x, w1, w2, sh, d0, dx, og, base, out_0, ou
         def load_base(p):
             nc.sync.dma_start(out=base_t[p][:], in_=feature_rows(base[p[1]], p))
 
-        nc.sync.dma_start(out=w_raw[0][:], in_=k_rows(w1))
         nc.sync.dma_start(out=w_raw[1][:], in_=k_rows(w2))
+        load_x(0, 0)
         nc.scalar.dma_start(out=sh_t[:], in_=sh.rearrange("g (q h) o -> q g (h o)", h=HALVES))
         nc.scalar.dma_start(out=og_t[:], in_=og.rearrange("g (q h) o -> q g (h o)", h=HALVES))
-        load_x(0, 0)
+        nc.sync.dma_start(out=w_raw[0][:], in_=k_rows(w1))
         load_x(0, 1)
         load_d0(pairs[0])
-        load_base(pairs[0])
-        load_d0(pairs[1])
         load_x(1, 0)
         load_x(1, 1)
+        load_d0(pairs[1])
+        load_d0(pairs[2])
+        load_base(pairs[0])
+        load_d0(pairs[3])
         load_base(pairs[1])
-        for p in pairs[2:]:
-            load_d0(p)
-            load_base(p)
+        load_base(pairs[2])
+        load_base(pairs[3])
 
         def round_w(i):
             nc.vector.tensor_copy(
@@ -104,41 +106,51 @@ def tile_rows_pl_tnkernrbf_kernel(tc, x, w1, w2, sh, d0, dx, og, base, out_0, ou
 
         def round_x(copy, c, i, lo, hi):
             copy(
-                out=x_bf[c][i][:, lo * PACK : hi * PACK].rearrange("p (a b j) -> p a j b", b=4, j=PACK),
-                in_=x_raw[c][i][:, :, lo:hi].rearrange("p j (a b) -> p a j b", b=4),
+                out=x_bf[c][i][:, lo * PACK : hi * PACK].rearrange("p (a b j) -> p a j b", b=2, j=PACK),
+                in_=x_raw[c][i][:, :, lo:hi].rearrange("p j (a b) -> p a j b", b=2),
             )
 
-        def quant_x(c, i):
+        def quant_x(c, i, lo=0, hi=W):
             nc.vector.quantize_mx(
-                out=x_codes[c][:, i * W : (i + 1) * W].bitcast(FP8X4),
-                scales=x_scales[c][:, i * W : (i + 1) * W],
-                in_=x_bf[c][i][:],
+                out=x_codes[c][i][:, lo:hi].bitcast(FP8X4),
+                scales=x_scales[c][i][:, lo:hi],
+                in_=x_bf[c][i][:, PACK * lo : PACK * hi],
             )
+
+        def pool_round(out, in_):
+            nc.gpsimd.tensor_scalar(out=out, in0=in_, scalar1=1.0, scalar2=0.0, op0=ALU.mult, op1=ALU.add)
 
         acc = {}
 
-        def matmul(c, g, h, i):
+        def bank_calls(c, g, i, j):
             rows = slice(g * ROWS, (g + 1) * ROWS)
-            feats = slice(h * P, (h + 1) * P)
-            bank = ps.tile([P, 2 * W], F32, name="acc%d%d%d" % (g, h, i))
-            acc[(c, g, h, i)] = bank
-            nc.tensor.matmul_mx(
-                out=bank[:],
-                lhsT=w_codes[i][rows, feats].bitcast(FP8X4),
-                lhsT_scale=w_scales[i][rows, feats],
-                rhs=x_codes[c][rows, :].bitcast(FP8X4),
-                rhs_scale=x_scales[c][rows, :],
-                start=True,
-                stop=True,
-            )
+            bank = ps.tile([P, HALVES, W], F32, name="acc%d%d%d" % (g, i, j))
+            acc[(c, g, i, j)] = bank
 
-        def copy_z2(p, h):
-            nc.scalar.copy(out=z2_t[p][:, h, :], in_=acc[p + (h, 1)][:, 0:W])
+            def call(h, n0):
+                nc.tensor.matmul_mx(
+                    out=bank[:, h, n0 : n0 + NT],
+                    lhsT=w_codes[i][rows, h * P : (h + 1) * P].bitcast(FP8X4),
+                    lhsT_scale=w_scales[i][rows, h * P : (h + 1) * P],
+                    rhs=x_codes[c][j][rows, n0 : n0 + NT].bitcast(FP8X4),
+                    rhs_scale=x_scales[c][j][rows, n0 : n0 + NT],
+                    start=True,
+                    stop=True,
+                )
 
-        def dist(p, h):
+            return [(call, h, n0) for n0 in range(0, W, NT) for h in range(HALVES)]
+
+        def matmuls(*banks):
+            for calls in zip(*[bank_calls(*bank) for bank in banks]):
+                for call, h, n0 in calls:
+                    call(h, n0)
+
+        def copy_z2(p):
+            nc.scalar.copy(out=z2_t[p][:], in_=acc[p + (1, 0)][:])
+
+        def dist(p):
             nc.vector.scalar_tensor_tensor(
-                out=q_t[p][:, h, :], in0=acc[p + (h, 0)][:, 0:W], scalar=2.0, in1=d0_t[p][:, h, :],
-                op0=ALU.mult, op1=ALU.subtract,
+                out=q_t[p][:], in0=acc[p + (0, 0)][:], scalar=2.0, in1=d0_t[p][:], op0=ALU.mult, op1=ALU.subtract
             )
 
         def expo(p, h):
@@ -146,50 +158,56 @@ def tile_rows_pl_tnkernrbf_kernel(tc, x, w1, w2, sh, d0, dx, og, base, out_0, ou
 
         def prod(p, h):
             nc.vector.scalar_tensor_tensor(
-                out=b_t[p][:, h, :], in0=acc[p + (h, 0)][:, W : 2 * W], scalar=k_t[:, p[1], h : h + 1],
+                out=b_t[p][:, h, :], in0=acc[p + (0, 1)][:, h, :], scalar=k_t[:, p[1], h : h + 1],
                 in1=z2_t[p][:, h, :], op0=ALU.mult, op1=ALU.mult,
             )
 
         def plus(p, h):
             nc.vector.scalar_tensor_tensor(
-                out=c_t[p][:, h, :], in0=acc[p + (h, 1)][:, W : 2 * W], scalar=og_t[:, p[1], h : h + 1],
+                out=c_t[p][:, h, :], in0=acc[p + (1, 1)][:, h, :], scalar=og_t[:, p[1], h : h + 1],
                 in1=b_t[p][:, h, :], op0=ALU.mult, op1=ALU.add,
             )
 
-        def weigh(p, lo=0, hi=W):
-            nc.vector.tensor_tensor(out=f_t[p][:, :, lo:hi], in0=c_t[p][:, :, lo:hi], in1=e_t[p][:, :, lo:hi], op=ALU.mult)
+        def weigh(engine, p, lo=0, hi=W, hs=slice(0, HALVES)):
+            engine.tensor_tensor(out=f_t[p][:, hs, lo:hi], in0=c_t[p][:, hs, lo:hi], in1=e_t[p][:, hs, lo:hi], op=ALU.mult)
 
-        def finish(p):
-            nc.vector.tensor_tensor(out=y_t[p][:], in0=f_t[p][:], in1=base_t[p][:], op=ALU.add)
+        def finish(engine, p):
+            engine.tensor_tensor(out=y_t[p][:], in0=f_t[p][:], in1=base_t[p][:], op=ALU.add)
 
         def finish_bf(p, lo, hi):
             nc.vector.tensor_tensor(
-                out=yb_t[p][:, lo * HALVES : hi * HALVES].rearrange("q (n h) -> q n h", h=HALVES),
-                in0=f_t[p][:, :, lo:hi].rearrange("q h n -> q n h"),
-                in1=base_t[p][:, :, lo:hi].rearrange("q h n -> q n h"),
+                out=yb_t[p][:, lo * HALVES : hi * HALVES].rearrange("q (a b h) -> q a h b", b=2, h=HALVES),
+                in0=f_t[p][:, :, lo:hi].rearrange("q h (a b) -> q a h b", b=2),
+                in1=base_t[p][:, :, lo:hi].rearrange("q h (a b) -> q a h b", b=2),
                 op=ALU.add,
             )
 
         def round_y(p):
             nc.scalar.copy(
-                out=yb_t[p][:].rearrange("q (n h) -> q n h", h=HALVES), in_=y_t[p][:].rearrange("q h n -> q n h")
+                out=yb_t[p][:].rearrange("q (a b h) -> q a h b", b=2, h=HALVES),
+                in_=y_t[p][:].rearrange("q h (a b) -> q a h b", b=2),
             )
 
         def store_y(p):
             nc.sync.dma_start(out=feature_rows(out_0[p[1] * M : (p[1] + 1) * M, :], p), in_=y_t[p][:])
 
-        def hop(p):
+        def hop(p, lo=0, hi=W):
             c, g = p
-            nc.sync.dma_start(out=hop_t[c][g * ROWS : (g + 1) * ROWS, :, :], in_=yb_t[p][:].bitcast(F32))
-
-        def regroup(copy, c):
-            copy(
-                out=yq_t[c][:].bitcast(F32).rearrange("p (n r) -> p n r", r=2),
-                in_=hop_t[c][:].rearrange("p r n -> p n r"),
+            nc.sync.dma_start(
+                out=hop_t[c][g * ROWS : (g + 1) * ROWS, :, lo:hi], in_=yb_t[p][:].bitcast(F32)[:, lo:hi]
             )
 
-        def quant_y(c):
-            nc.vector.quantize_mx(out=y_codes[:, cols(c)].bitcast(FP8X4), scales=y_scales[:, cols(c)], in_=yq_t[c][:])
+        def regroup(copy, c, lo=0, hi=W):
+            copy(
+                out=yq_t[c][:].bitcast(F32)[:, 2 * lo : 2 * hi].rearrange("p (a b r) -> p a r b", b=2, r=2),
+                in_=hop_t[c][:, :, lo:hi].rearrange("p r (a b) -> p a r b", b=2),
+            )
+
+        def quant_y(c, lo=0, hi=W):
+            at = slice(c * W + lo, c * W + hi)
+            nc.vector.quantize_mx(
+                out=y_codes[:, at].bitcast(FP8X4), scales=y_scales[:, at], in_=yq_t[c][:, PACK * lo : PACK * hi]
+            )
 
         def store_words(c):
             nc.sync.dma_start(
@@ -204,95 +222,98 @@ def tile_rows_pl_tnkernrbf_kernel(tc, x, w1, w2, sh, d0, dx, og, base, out_0, ou
             )
 
         p0, p1, p2, p3 = pairs
+        H = W // 2
 
-        round_w(0)
-        quant_w(0)
         round_w(1)
-        nc.vector.scalar_tensor_tensor(out=k_t[:], in0=sh_t[:], scalar=2.0, in1=og_t[:], op0=ALU.mult, op1=ALU.mult)
         quant_w(1)
         round_x(nc.vector.tensor_copy, 0, 0, 0, W)
         quant_x(0, 0)
-        round_x(nc.vector.tensor_copy, 0, 1, 0, SPLIT)
-        round_x(nc.scalar.copy, 0, 1, SPLIT, W)
-        quant_x(0, 1)
-        for g, h, i in [(0, 0, 1), (0, 0, 0), (0, 1, 1), (1, 0, 1), (0, 1, 0), (1, 0, 0), (1, 1, 1), (1, 1, 0)]:
-            matmul(0, g, h, i)
-
-        copy_z2(p0, 0)
-        dist(p0, 0)
-        prod(p0, 0)
+        matmuls((0, 0, 1, 0))
+        matmuls((0, 1, 1, 0))
+        round_w(0)
+        nc.vector.scalar_tensor_tensor(out=k_t[:], in0=sh_t[:], scalar=2.0, in1=og_t[:], op0=ALU.mult, op1=ALU.mult)
+        quant_w(0)
+        matmuls((0, 0, 0, 0))
+        matmuls((0, 1, 0, 0))
+        round_x(nc.vector.tensor_copy, 0, 1, 0, NT)
+        round_x(nc.scalar.copy, 0, 1, NT, W)
+        copy_z2(p0)
+        copy_z2(p1)
+        quant_x(0, 1, 0, NT)
+        quant_x(0, 1, NT, W)
+        for g in range(G):
+            matmuls((0, g, 0, 1))
+            matmuls((0, g, 1, 1))
+        dist(p0)
+        round_x(nc.scalar.copy, 1, 0, 0, W)
         expo(p0, 0)
-        copy_z2(p0, 1)
-        plus(p0, 0)
-        dist(p0, 1)
-        prod(p0, 1)
-        round_x(nc.scalar.copy, 1, 0, 0, W // 2)
         expo(p0, 1)
-        copy_z2(p1, 0)
-        dist(p1, 0)
+        prod(p0, 0)
+        prod(p0, 1)
+        plus(p0, 0)
         plus(p0, 1)
-        round_x(nc.scalar.copy, 1, 0, W // 2, W)
-        copy_z2(p1, 1)
-        dist(p1, 1)
-        weigh(p0)
+        weigh(nc.gpsimd, p0)
         prod(p1, 0)
-        finish(p0)
-        store_y(p0)
-        round_x(nc.scalar.copy, 1, 1, 0, W // 2)
-        expo(p1, 0)
-        round_x(nc.scalar.copy, 1, 1, W // 2, W)
-        expo(p1, 1)
-        quant_x(1, 0)
         prod(p1, 1)
+        quant_x(1, 0)
+        matmuls((1, 0, 1, 0))
+        matmuls((1, 0, 0, 0))
+        matmuls((1, 1, 1, 0))
+        round_x(nc.scalar.copy, 1, 1, 0, W)
         plus(p1, 0)
-        quant_x(1, 1)
         plus(p1, 1)
-        for g, h, i in [(0, 0, 1), (0, 0, 0), (0, 1, 1), (1, 0, 1), (0, 1, 0), (1, 0, 0), (1, 1, 1), (1, 1, 0)]:
-            matmul(1, g, h, i)
+        dist(p1)
+        copy_z2(p2)
+        expo(p1, 0)
+        expo(p1, 1)
+        quant_x(1, 1)
+        matmuls((1, 0, 0, 1))
+        matmuls((1, 0, 1, 1))
+        matmuls((1, 1, 0, 0))
+        matmuls((1, 1, 0, 1))
+        matmuls((1, 1, 1, 1))
+        finish(nc.vector, p0)
+        store_y(p0)
+        weigh(nc.gpsimd, p1)
+        finish(nc.gpsimd, p1)
+        dist(p2)
+        copy_z2(p3)
+        expo(p2, 0)
+        expo(p2, 1)
         round_y(p0)
         hop(p0)
-        weigh(p1)
-        copy_z2(p2, 0)
-        dist(p2, 0)
-        finish(p1)
-        store_y(p1)
-        expo(p2, 0)
-        copy_z2(p2, 1)
         prod(p2, 0)
-        dist(p2, 1)
-        plus(p2, 0)
-        expo(p2, 1)
-        round_y(p1)
-        hop(p1)
         prod(p2, 1)
-        copy_z2(p3, 0)
-        copy_z2(p3, 1)
-        dist(p3, 0)
+        plus(p2, 0)
         plus(p2, 1)
-        dist(p3, 1)
+        dist(p3)
         expo(p3, 0)
         expo(p3, 1)
-        weigh(p2)
+        round_y(p1)
+        hop(p1)
         prod(p3, 0)
-        finish(p2)
-        store_y(p2)
-        round_y(p2)
-        hop(p2)
-        regroup(nc.scalar.copy, 0)
         prod(p3, 1)
         plus(p3, 0)
         plus(p3, 1)
+        for lo in (0, H):
+            weigh(nc.vector, p2, lo, lo + H)
+            weigh(nc.vector, p3, lo, lo + H)
+            finish_bf(p2, lo, lo + H)
+            hop(p2, lo, lo + H)
+            finish_bf(p3, lo, lo + H)
+            hop(p3, lo, lo + H)
+        store_y(p1)
+        finish(nc.vector, p2)
+        store_y(p2)
+        finish(nc.vector, p3)
+        store_y(p3)
+        regroup(nc.scalar.copy, 0)
         quant_y(0)
         store_words(0)
-        weigh(p3, 0, W // 2)
-        weigh(p3, W // 2, W)
-        finish_bf(p3, 0, W // 2)
-        finish_bf(p3, W // 2, W)
-        hop(p3)
-        finish(p3)
-        store_y(p3)
-        regroup(nc.vector.tensor_copy, 1)
-        quant_y(1)
+        regroup(nc.scalar.copy, 1, 0, H)
+        quant_y(1, 0, H)
+        regroup(nc.vector.tensor_copy, 1, H, W)
+        quant_y(1, H, W)
         store_words(1)
         for quad in range(4):
             store_scales((nc.scalar, nc.sync)[quad % 2], quad)

@@ -17,11 +17,14 @@ EXP = mybir.ActivationFunctionType.Exp
 P = 128
 PACK = 4
 ROWS = D // PACK
-HALVES = M // P
+PER = M // P
 CHUNKS = 2
 W = N // CHUNKS
-SPLIT = 160
 NT = 128
+RUN = 2
+QUAD = 32
+W1, W2 = 0, 1
+X, DX = 0, 1
 
 
 def tile_rows_pl_tnkernrbf_kernel(tc, x, w1, w2, sh, d0, dx, og, base, out_0, out_1, out_2):
@@ -37,77 +40,71 @@ def tile_rows_pl_tnkernrbf_kernel(tc, x, w1, w2, sh, d0, dx, og, base, out_0, ou
         def cols(c):
             return slice(c * W, (c + 1) * W)
 
-        pairs = [(c, g) for c in range(CHUNKS) for g in range(G)]
+        parts = [(c, g) for c in range(CHUNKS) for g in range(G)]
 
-        w_raw = [tile("w_raw%d" % i, [P, PACK, M], F32) for i in range(2)]
-        w_bf = [tile("w_bf%d" % i, [P, M * PACK], BF16) for i in range(2)]
-        w_codes = [tile("w_codes%d" % i, [P, M], U32) for i in range(2)]
-        w_scales = [tile("w_scales%d" % i, [P, M], U8) for i in range(2)]
-        x_raw = [[tile("x_raw%d%d" % (c, i), [P, PACK, W], F32) for i in range(2)] for c in range(CHUNKS)]
-        x_bf = [[tile("x_bf%d%d" % (c, i), [P, W * PACK], BF16) for i in range(2)] for c in range(CHUNKS)]
-        x_codes = [[tile("x_codes%d%d" % (c, i), [P, W], U32) for i in range(2)] for c in range(CHUNKS)]
-        x_scales = [[tile("x_scales%d%d" % (c, i), [P, W], U8) for i in range(2)] for c in range(CHUNKS)]
-        sh_t = tile("sh_t", [P, G, HALVES], F32)
-        og_t = tile("og_t", [P, G, HALVES], F32)
-        k_t = tile("k_t", [P, G, HALVES], F32)
+        def part_tiles(name, shape, dtype):
+            return dict((part, tile("%s%d%d" % ((name,) + part), shape, dtype)) for part in parts)
 
-        def per_pair(name):
-            return dict((p, tile("%s%d%d" % (name, p[0], p[1]), [P, HALVES, W], F32)) for p in pairs)
+        def operand_tiles(name, shape, dtype):
+            return [[tile("%s%d%d" % (name, c, i), shape, dtype) for i in (X, DX)] for c in range(CHUNKS)]
 
-        d0_t, base_t = per_pair("d0"), per_pair("base")
-        q_t, e_t, z2_t, b_t, c_t, f_t, y_t = [per_pair(s) for s in ("q", "e", "z2", "b", "c", "f", "y")]
-        yb_t = dict((p, tile("yb%d%d" % p, [P, W * HALVES], BF16)) for p in pairs)
-        hop_t = [tile("hop%d" % c, [P, 2, W], F32) for c in range(CHUNKS)]
+        w_raw = [tile("w_raw%d" % i, [P, PACK, M], F32) for i in (W1, W2)]
+        w_bf = [tile("w_bf%d" % i, [P, M * PACK], BF16) for i in (W1, W2)]
+        w_codes = [tile("w_codes%d" % i, [P, M], U32) for i in (W1, W2)]
+        w_scales = [tile("w_scales%d" % i, [P, M], U8) for i in (W1, W2)]
+        x_raw = operand_tiles("x_raw", [P, PACK, W], F32)
+        x_bf = operand_tiles("x_bf", [P, W * PACK], BF16)
+        x_codes = operand_tiles("x_codes", [P, W], U32)
+        x_scales = operand_tiles("x_scales", [P, W], U8)
+        sh_t = tile("sh_t", [P, G, PER], F32)
+        og_t = tile("og_t", [P, G, PER], F32)
+        k_t = tile("k_t", [P, G, PER], F32)
+        d0_t = part_tiles("d0", [P, PER, W], F32)
+        base_t = part_tiles("base", [P, PER, W], F32)
+        q_t = part_tiles("q", [P, PER, W], F32)
+        e_t = part_tiles("e", [P, PER, W], F32)
+        z2_t = part_tiles("z2", [P, PER, W], F32)
+        b_t = part_tiles("b", [P, PER, W], F32)
+        c_t = part_tiles("c", [P, PER, W], F32)
+        f_t = part_tiles("f", [P, PER, W], F32)
+        y_t = part_tiles("y", [P, PER, W], F32)
+        yb_t = part_tiles("yb", [P, W * PER], BF16)
+        moved_t = [tile("moved%d" % c, [P, 2, W], F32) for c in range(CHUNKS)]
         yq_t = [tile("yq%d" % c, [P, W * PACK], BF16) for c in range(CHUNKS)]
         y_codes = tile("y_codes", [P, N], U32)
         y_scales = tile("y_scales", [P, N], U8)
 
-        def k_rows(t):
+        def d_rows(t):
             return t.rearrange("g (p j) n -> (g p) j n", j=PACK)
 
-        def feature_rows(t, p):
-            c, g = p
-            return t.rearrange("(q h) n -> q h n", h=HALVES)[:, :, cols(c)]
+        def feature_rows(t, c):
+            return t.rearrange("(q h) n -> q h n", h=PER)[:, :, cols(c)]
+
+        def load_w(i):
+            nc.sync.dma_start(out=w_raw[i][:], in_=d_rows((w1, w2)[i]))
 
         def load_x(c, i):
-            nc.sync.dma_start(out=x_raw[c][i][:], in_=k_rows((x, dx)[i])[:, :, cols(c)])
+            nc.sync.dma_start(out=x_raw[c][i][:], in_=d_rows((x, dx)[i])[:, :, cols(c)])
 
-        def load_d0(p):
-            nc.sync.dma_start(out=d0_t[p][:], in_=feature_rows(d0[p[1]], p))
+        def load_d0(part):
+            nc.sync.dma_start(out=d0_t[part][:], in_=feature_rows(d0[part[1]], part[0]))
 
-        def load_base(p):
-            nc.sync.dma_start(out=base_t[p][:], in_=feature_rows(base[p[1]], p))
-
-        nc.sync.dma_start(out=w_raw[1][:], in_=k_rows(w2))
-        load_x(0, 0)
-        nc.scalar.dma_start(out=sh_t[:], in_=sh.rearrange("g (q h) o -> q g (h o)", h=HALVES))
-        nc.scalar.dma_start(out=og_t[:], in_=og.rearrange("g (q h) o -> q g (h o)", h=HALVES))
-        nc.sync.dma_start(out=w_raw[0][:], in_=k_rows(w1))
-        load_x(0, 1)
-        load_d0(pairs[0])
-        load_x(1, 0)
-        load_x(1, 1)
-        load_d0(pairs[1])
-        load_d0(pairs[2])
-        load_base(pairs[0])
-        load_d0(pairs[3])
-        load_base(pairs[1])
-        load_base(pairs[2])
-        load_base(pairs[3])
+        def load_base(part):
+            nc.sync.dma_start(out=base_t[part][:], in_=feature_rows(base[part[1]], part[0]))
 
         def round_w(i):
             nc.vector.tensor_copy(
-                out=w_bf[i][:].rearrange("p (h q j) -> p q j h", h=HALVES, j=PACK),
-                in_=w_raw[i][:].rearrange("p j (q h) -> p q j h", h=HALVES),
+                out=w_bf[i][:].rearrange("p (h q j) -> p q j h", h=PER, j=PACK),
+                in_=w_raw[i][:].rearrange("p j (q h) -> p q j h", h=PER),
             )
 
         def quant_w(i):
             nc.vector.quantize_mx(out=w_codes[i][:].bitcast(FP8X4), scales=w_scales[i][:], in_=w_bf[i][:])
 
-        def round_x(copy, c, i, lo, hi):
+        def round_x(copy, c, i, lo=0, hi=W):
             copy(
-                out=x_bf[c][i][:, lo * PACK : hi * PACK].rearrange("p (a b j) -> p a j b", b=2, j=PACK),
-                in_=x_raw[c][i][:, :, lo:hi].rearrange("p j (a b) -> p a j b", b=2),
+                out=x_bf[c][i][:, lo * PACK : hi * PACK].rearrange("p (a b j) -> p a j b", b=RUN, j=PACK),
+                in_=x_raw[c][i][:, :, lo:hi].rearrange("p j (a b) -> p a j b", b=RUN),
             )
 
         def quant_x(c, i, lo=0, hi=W):
@@ -117,90 +114,90 @@ def tile_rows_pl_tnkernrbf_kernel(tc, x, w1, w2, sh, d0, dx, og, base, out_0, ou
                 in_=x_bf[c][i][:, PACK * lo : PACK * hi],
             )
 
-        def pool_round(out, in_):
-            nc.gpsimd.tensor_scalar(out=out, in0=in_, scalar1=1.0, scalar2=0.0, op0=ALU.mult, op1=ALU.add)
-
         acc = {}
 
-        def bank_calls(c, g, i, j):
-            rows = slice(g * ROWS, (g + 1) * ROWS)
-            bank = ps.tile([P, HALVES, W], F32, name="acc%d%d%d" % (g, i, j))
-            acc[(c, g, i, j)] = bank
+        def product(c, i, j):
+            for g in range(G):
+                acc[(c, g, i, j)] = ps.tile([P, PER, W], F32, name="acc%d%d%d" % (g, i, j))
+            for n0 in range(0, W, NT):
+                for h in range(PER):
+                    for g in range(G):
+                        rows = slice(g * ROWS, (g + 1) * ROWS)
+                        nc.tensor.matmul_mx(
+                            out=acc[(c, g, i, j)][:, h, n0 : n0 + NT],
+                            lhsT=w_codes[i][rows, h * P : (h + 1) * P].bitcast(FP8X4),
+                            lhsT_scale=w_scales[i][rows, h * P : (h + 1) * P],
+                            rhs=x_codes[c][j][rows, n0 : n0 + NT].bitcast(FP8X4),
+                            rhs_scale=x_scales[c][j][rows, n0 : n0 + NT],
+                            start=True,
+                            stop=True,
+                        )
 
-            def call(h, n0):
-                nc.tensor.matmul_mx(
-                    out=bank[:, h, n0 : n0 + NT],
-                    lhsT=w_codes[i][rows, h * P : (h + 1) * P].bitcast(FP8X4),
-                    lhsT_scale=w_scales[i][rows, h * P : (h + 1) * P],
-                    rhs=x_codes[c][j][rows, n0 : n0 + NT].bitcast(FP8X4),
-                    rhs_scale=x_scales[c][j][rows, n0 : n0 + NT],
-                    start=True,
-                    stop=True,
+        def copy_z2(part):
+            nc.scalar.copy(out=z2_t[part][:], in_=acc[part + (W2, X)][:])
+
+        def step_q(part):
+            nc.vector.scalar_tensor_tensor(
+                out=q_t[part][:], in0=acc[part + (W1, X)][:], scalar=2.0, in1=d0_t[part][:],
+                op0=ALU.mult, op1=ALU.subtract,
+            )
+
+        def step_e(part):
+            for h in range(PER):
+                nc.scalar.activation(
+                    out=e_t[part][:, h, :], in_=q_t[part][:, h, :], func=EXP, scale=sh_t[:, part[1], h : h + 1]
                 )
 
-            return [(call, h, n0) for n0 in range(0, W, NT) for h in range(HALVES)]
+        def step_b(part):
+            for h in range(PER):
+                nc.vector.scalar_tensor_tensor(
+                    out=b_t[part][:, h, :], in0=acc[part + (W1, DX)][:, h, :], scalar=k_t[:, part[1], h : h + 1],
+                    in1=z2_t[part][:, h, :], op0=ALU.mult, op1=ALU.mult,
+                )
 
-        def matmuls(*banks):
-            for calls in zip(*[bank_calls(*bank) for bank in banks]):
-                for call, h, n0 in calls:
-                    call(h, n0)
+        def step_c(part, features=range(PER)):
+            for h in features:
+                nc.vector.scalar_tensor_tensor(
+                    out=c_t[part][:, h, :], in0=acc[part + (W2, DX)][:, h, :], scalar=og_t[:, part[1], h : h + 1],
+                    in1=b_t[part][:, h, :], op0=ALU.mult, op1=ALU.add,
+                )
 
-        def copy_z2(p):
-            nc.scalar.copy(out=z2_t[p][:], in_=acc[p + (1, 0)][:])
-
-        def dist(p):
-            nc.vector.scalar_tensor_tensor(
-                out=q_t[p][:], in0=acc[p + (0, 0)][:], scalar=2.0, in1=d0_t[p][:], op0=ALU.mult, op1=ALU.subtract
+        def step_f(engine, part, lo=0, hi=W):
+            engine.tensor_tensor(
+                out=f_t[part][:, :, lo:hi], in0=c_t[part][:, :, lo:hi], in1=e_t[part][:, :, lo:hi], op=ALU.mult
             )
 
-        def expo(p, h):
-            nc.scalar.activation(out=e_t[p][:, h, :], in_=q_t[p][:, h, :], func=EXP, scale=sh_t[:, p[1], h : h + 1])
+        def step_y(engine, part):
+            engine.tensor_tensor(out=y_t[part][:], in0=f_t[part][:], in1=base_t[part][:], op=ALU.add)
 
-        def prod(p, h):
-            nc.vector.scalar_tensor_tensor(
-                out=b_t[p][:, h, :], in0=acc[p + (0, 1)][:, h, :], scalar=k_t[:, p[1], h : h + 1],
-                in1=z2_t[p][:, h, :], op0=ALU.mult, op1=ALU.mult,
+        def store_y(part):
+            c, g = part
+            nc.sync.dma_start(out=feature_rows(out_0[g * M : (g + 1) * M, :], c), in_=y_t[part][:])
+
+        def round_y(part):
+            nc.scalar.copy(
+                out=yb_t[part][:].rearrange("q (a b h) -> q a h b", b=RUN, h=PER),
+                in_=y_t[part][:].rearrange("q h (a b) -> q a h b", b=RUN),
             )
 
-        def plus(p, h):
-            nc.vector.scalar_tensor_tensor(
-                out=c_t[p][:, h, :], in0=acc[p + (1, 1)][:, h, :], scalar=og_t[:, p[1], h : h + 1],
-                in1=b_t[p][:, h, :], op0=ALU.mult, op1=ALU.add,
-            )
-
-        def weigh(engine, p, lo=0, hi=W, hs=slice(0, HALVES)):
-            engine.tensor_tensor(out=f_t[p][:, hs, lo:hi], in0=c_t[p][:, hs, lo:hi], in1=e_t[p][:, hs, lo:hi], op=ALU.mult)
-
-        def finish(engine, p):
-            engine.tensor_tensor(out=y_t[p][:], in0=f_t[p][:], in1=base_t[p][:], op=ALU.add)
-
-        def finish_bf(p, lo, hi):
+        def step_y_rounded(part, lo, hi):
             nc.vector.tensor_tensor(
-                out=yb_t[p][:, lo * HALVES : hi * HALVES].rearrange("q (a b h) -> q a h b", b=2, h=HALVES),
-                in0=f_t[p][:, :, lo:hi].rearrange("q h (a b) -> q a h b", b=2),
-                in1=base_t[p][:, :, lo:hi].rearrange("q h (a b) -> q a h b", b=2),
+                out=yb_t[part][:, lo * PER : hi * PER].rearrange("q (a b h) -> q a h b", b=RUN, h=PER),
+                in0=f_t[part][:, :, lo:hi].rearrange("q h (a b) -> q a h b", b=RUN),
+                in1=base_t[part][:, :, lo:hi].rearrange("q h (a b) -> q a h b", b=RUN),
                 op=ALU.add,
             )
 
-        def round_y(p):
-            nc.scalar.copy(
-                out=yb_t[p][:].rearrange("q (a b h) -> q a h b", b=2, h=HALVES),
-                in_=y_t[p][:].rearrange("q h (a b) -> q a h b", b=2),
-            )
-
-        def store_y(p):
-            nc.sync.dma_start(out=feature_rows(out_0[p[1] * M : (p[1] + 1) * M, :], p), in_=y_t[p][:])
-
-        def hop(p, lo=0, hi=W):
-            c, g = p
+        def move_y(part, lo=0, hi=W):
+            c, g = part
             nc.sync.dma_start(
-                out=hop_t[c][g * ROWS : (g + 1) * ROWS, :, lo:hi], in_=yb_t[p][:].bitcast(F32)[:, lo:hi]
+                out=moved_t[c][g * ROWS : (g + 1) * ROWS, :, lo:hi], in_=yb_t[part][:].bitcast(F32)[:, lo:hi]
             )
 
-        def regroup(copy, c, lo=0, hi=W):
+        def pack_y(copy, c, lo=0, hi=W):
             copy(
-                out=yq_t[c][:].bitcast(F32)[:, 2 * lo : 2 * hi].rearrange("p (a b r) -> p a r b", b=2, r=2),
-                in_=hop_t[c][:, :, lo:hi].rearrange("p r (a b) -> p a r b", b=2),
+                out=yq_t[c][:].bitcast(F32)[:, 2 * lo : 2 * hi].rearrange("p (a b r) -> p a r b", b=RUN, r=2),
+                in_=moved_t[c][:, :, lo:hi].rearrange("p r (a b) -> p a r b", b=RUN),
             )
 
         def quant_y(c, lo=0, hi=W):
@@ -218,102 +215,100 @@ def tile_rows_pl_tnkernrbf_kernel(tc, x, w1, w2, sh, d0, dx, og, base, out_0, ou
         def store_scales(queue, quad):
             queue.dma_start(
                 out=out_2[0, 4 * quad : 4 * quad + 4, :].bitcast(I32),
-                in_=y_scales[32 * quad : 32 * quad + 4, :].bitcast(I32),
+                in_=y_scales[QUAD * quad : QUAD * quad + 4, :].bitcast(I32),
             )
 
-        p0, p1, p2, p3 = pairs
-        H = W // 2
+        first0, first1, last0, last1 = parts
 
-        round_w(1)
-        quant_w(1)
-        round_x(nc.vector.tensor_copy, 0, 0, 0, W)
-        quant_x(0, 0)
-        matmuls((0, 0, 1, 0))
-        matmuls((0, 1, 1, 0))
-        round_w(0)
+        load_w(W2)
+        load_x(0, X)
+        for vec, vec_t in ((sh, sh_t), (og, og_t)):
+            nc.scalar.dma_start(out=vec_t[:], in_=vec.rearrange("g (q h) o -> q g (h o)", h=PER))
+        load_w(W1)
+        load_x(0, DX)
+        load_d0(first0)
+        load_x(1, X)
+        load_x(1, DX)
+        load_d0(first1)
+        load_d0(last0)
+        load_base(first0)
+        load_d0(last1)
+        for part in (first1, last0, last1):
+            load_base(part)
+
+        round_w(W2)
+        quant_w(W2)
+        round_x(nc.vector.tensor_copy, 0, X)
+        quant_x(0, X)
+        product(0, W2, X)
+        round_w(W1)
         nc.vector.scalar_tensor_tensor(out=k_t[:], in0=sh_t[:], scalar=2.0, in1=og_t[:], op0=ALU.mult, op1=ALU.mult)
-        quant_w(0)
-        matmuls((0, 0, 0, 0))
-        matmuls((0, 1, 0, 0))
-        round_x(nc.vector.tensor_copy, 0, 1, 0, NT)
-        round_x(nc.scalar.copy, 0, 1, NT, W)
-        copy_z2(p0)
-        copy_z2(p1)
-        quant_x(0, 1, 0, NT)
-        quant_x(0, 1, NT, W)
-        for g in range(G):
-            matmuls((0, g, 0, 1))
-            matmuls((0, g, 1, 1))
-        dist(p0)
-        round_x(nc.scalar.copy, 1, 0, 0, W)
-        expo(p0, 0)
-        expo(p0, 1)
-        prod(p0, 0)
-        prod(p0, 1)
-        plus(p0, 0)
-        plus(p0, 1)
-        weigh(nc.gpsimd, p0)
-        prod(p1, 0)
-        prod(p1, 1)
-        quant_x(1, 0)
-        matmuls((1, 0, 1, 0))
-        matmuls((1, 0, 0, 0))
-        matmuls((1, 1, 1, 0))
-        round_x(nc.scalar.copy, 1, 1, 0, W)
-        plus(p1, 0)
-        plus(p1, 1)
-        dist(p1)
-        copy_z2(p2)
-        expo(p1, 0)
-        expo(p1, 1)
-        quant_x(1, 1)
-        matmuls((1, 0, 0, 1))
-        matmuls((1, 0, 1, 1))
-        matmuls((1, 1, 0, 0))
-        matmuls((1, 1, 0, 1))
-        matmuls((1, 1, 1, 1))
-        finish(nc.vector, p0)
-        store_y(p0)
-        weigh(nc.gpsimd, p1)
-        finish(nc.gpsimd, p1)
-        dist(p2)
-        copy_z2(p3)
-        expo(p2, 0)
-        expo(p2, 1)
-        round_y(p0)
-        hop(p0)
-        prod(p2, 0)
-        prod(p2, 1)
-        plus(p2, 0)
-        plus(p2, 1)
-        dist(p3)
-        expo(p3, 0)
-        expo(p3, 1)
-        round_y(p1)
-        hop(p1)
-        prod(p3, 0)
-        prod(p3, 1)
-        plus(p3, 0)
-        plus(p3, 1)
-        for lo in (0, H):
-            weigh(nc.vector, p2, lo, lo + H)
-            weigh(nc.vector, p3, lo, lo + H)
-            finish_bf(p2, lo, lo + H)
-            hop(p2, lo, lo + H)
-            finish_bf(p3, lo, lo + H)
-            hop(p3, lo, lo + H)
-        store_y(p1)
-        finish(nc.vector, p2)
-        store_y(p2)
-        finish(nc.vector, p3)
-        store_y(p3)
-        regroup(nc.scalar.copy, 0)
+        quant_w(W1)
+        product(0, W1, X)
+        round_x(nc.vector.tensor_copy, 0, DX, 0, NT)
+        round_x(nc.scalar.copy, 0, DX, NT, W)
+        copy_z2(first0)
+        copy_z2(first1)
+        quant_x(0, DX, 0, NT)
+        quant_x(0, DX, NT, W)
+        product(0, W1, DX)
+        product(0, W2, DX)
+
+        step_q(first0)
+        round_x(nc.scalar.copy, 1, X)
+        step_e(first0)
+        step_b(first0)
+        step_b(first1)
+        step_c(first0, [0])
+        quant_x(1, X)
+        step_c(first0, [1])
+        step_f(nc.gpsimd, first0)
+        product(1, W2, X)
+        round_x(nc.scalar.copy, 1, DX)
+        step_c(first1)
+        step_q(first1)
+        product(1, W1, X)
+        copy_z2(last0)
+        step_e(first1)
+        quant_x(1, DX)
+        product(1, W1, DX)
+        product(1, W2, DX)
+
+        step_y(nc.vector, first0)
+        store_y(first0)
+        step_f(nc.gpsimd, first1)
+        step_y(nc.gpsimd, first1)
+        step_q(last0)
+        copy_z2(last1)
+        step_e(last0)
+        round_y(first0)
+        move_y(first0)
+        step_q(last1)
+        step_e(last1)
+        step_b(last0)
+        step_b(last1)
+        round_y(first1)
+        move_y(first1)
+        step_c(last0)
+        step_c(last1)
+
+        halves = [(0, W // 2), (W // 2, W)]
+        for lo, hi in halves:
+            for part in (last0, last1):
+                step_f(nc.vector, part, lo, hi)
+            for part in (last0, last1):
+                step_y_rounded(part, lo, hi)
+                move_y(part, lo, hi)
+        store_y(first1)
+        for part in (last0, last1):
+            step_y(nc.vector, part)
+            store_y(part)
+        pack_y(nc.vector.tensor_copy, 0)
         quant_y(0)
         store_words(0)
-        regroup(nc.scalar.copy, 1, 0, H)
-        quant_y(1, 0, H)
-        regroup(nc.vector.tensor_copy, 1, H, W)
-        quant_y(1, H, W)
+        for copy, (lo, hi) in zip((nc.scalar.copy, nc.vector.tensor_copy), halves):
+            pack_y(copy, 1, lo, hi)
+            quant_y(1, lo, hi)
         store_words(1)
-        for quad in range(4):
+        for quad in range(P // QUAD):
             store_scales((nc.scalar, nc.sync)[quad % 2], quad)

from contextlib import ExitStack

import concourse.mybir as mybir

G, D, M, N = 2, 256, 256, 512
FLOPS = 4 * 2 * G * D * M * N

F32 = mybir.dt.float32
BF16 = mybir.dt.bfloat16
I32 = mybir.dt.int32
U32 = mybir.dt.uint32
U8 = mybir.dt.uint8
FP8X4 = mybir.dt.float8_e4m3fn_x4
ALU = mybir.AluOpType
EXP = mybir.ActivationFunctionType.Exp

P = 128
PACK = 4
ROWS = D // PACK
PER = M // P
CHUNKS = 2
W = N // CHUNKS
NT = 128
RUN = 2
QUAD = 32
W1, W2 = 0, 1
X, DX = 0, 1


def tile_rows_pl_tnkernrbf_kernel(tc, x, w1, w2, sh, d0, dx, og, base, out_0, out_1, out_2):
    nc = tc.nc
    with ExitStack() as ctx:
        sb = ctx.enter_context(tc.tile_pool(name="sb", bufs=1))
        ps = ctx.enter_context(tc.psum_pool(name="ps", bufs=1))
        ctx.enter_context(tc.manual_schedule())

        def tile(name, shape, dtype):
            return sb.tile(shape, dtype, name=name, align_bytes=64)

        def cols(c):
            return slice(c * W, (c + 1) * W)

        parts = [(c, g) for c in range(CHUNKS) for g in range(G)]

        def part_tiles(name, shape, dtype):
            return dict((part, tile("%s%d%d" % ((name,) + part), shape, dtype)) for part in parts)

        def operand_tiles(name, shape, dtype):
            return [[tile("%s%d%d" % (name, c, i), shape, dtype) for i in (X, DX)] for c in range(CHUNKS)]

        w_raw = [tile("w_raw%d" % i, [P, PACK, M], F32) for i in (W1, W2)]
        w_bf = [tile("w_bf%d" % i, [P, M * PACK], BF16) for i in (W1, W2)]
        w_codes = [tile("w_codes%d" % i, [P, M], U32) for i in (W1, W2)]
        w_scales = [tile("w_scales%d" % i, [P, M], U8) for i in (W1, W2)]
        x_raw = operand_tiles("x_raw", [P, PACK, W], F32)
        x_bf = operand_tiles("x_bf", [P, W * PACK], BF16)
        x_codes = operand_tiles("x_codes", [P, W], U32)
        x_scales = operand_tiles("x_scales", [P, W], U8)
        sh_t = tile("sh_t", [P, G, PER], F32)
        og_t = tile("og_t", [P, G, PER], F32)
        k_t = tile("k_t", [P, G, PER], F32)
        d0_t = part_tiles("d0", [P, PER, W], F32)
        base_t = part_tiles("base", [P, PER, W], F32)
        q_t = part_tiles("q", [P, PER, W], F32)
        e_t = part_tiles("e", [P, PER, W], F32)
        z2_t = part_tiles("z2", [P, PER, W], F32)
        b_t = part_tiles("b", [P, PER, W], F32)
        c_t = part_tiles("c", [P, PER, W], F32)
        f_t = part_tiles("f", [P, PER, W], F32)
        y_t = part_tiles("y", [P, PER, W], F32)
        yb_t = part_tiles("yb", [P, W * PER], BF16)
        moved_t = [tile("moved%d" % c, [P, 2, W], F32) for c in range(CHUNKS)]
        yq_t = [tile("yq%d" % c, [P, W * PACK], BF16) for c in range(CHUNKS)]
        y_codes = tile("y_codes", [P, N], U32)
        y_scales = tile("y_scales", [P, N], U8)

        def d_rows(t):
            return t.rearrange("g (p j) n -> (g p) j n", j=PACK)

        def feature_rows(t, c):
            return t.rearrange("(q h) n -> q h n", h=PER)[:, :, cols(c)]

        def load_w(i):
            nc.sync.dma_start(out=w_raw[i][:], in_=d_rows((w1, w2)[i]))

        def load_x(c, i):
            nc.sync.dma_start(out=x_raw[c][i][:], in_=d_rows((x, dx)[i])[:, :, cols(c)])

        def load_d0(part):
            nc.sync.dma_start(out=d0_t[part][:], in_=feature_rows(d0[part[1]], part[0]))

        def load_base(part):
            nc.sync.dma_start(out=base_t[part][:], in_=feature_rows(base[part[1]], part[0]))

        def round_w(i):
            nc.vector.tensor_copy(
                out=w_bf[i][:].rearrange("p (h q j) -> p q j h", h=PER, j=PACK),
                in_=w_raw[i][:].rearrange("p j (q h) -> p q j h", h=PER),
            )

        def quant_w(i):
            nc.vector.quantize_mx(out=w_codes[i][:].bitcast(FP8X4), scales=w_scales[i][:], in_=w_bf[i][:])

        def round_x(copy, c, i, lo=0, hi=W):
            copy(
                out=x_bf[c][i][:, lo * PACK : hi * PACK].rearrange("p (a b j) -> p a j b", b=RUN, j=PACK),
                in_=x_raw[c][i][:, :, lo:hi].rearrange("p j (a b) -> p a j b", b=RUN),
            )

        def quant_x(c, i, lo=0, hi=W):
            nc.vector.quantize_mx(
                out=x_codes[c][i][:, lo:hi].bitcast(FP8X4),
                scales=x_scales[c][i][:, lo:hi],
                in_=x_bf[c][i][:, PACK * lo : PACK * hi],
            )

        acc = {}

        def product(c, i, j):
            for g in range(G):
                acc[(c, g, i, j)] = ps.tile([P, PER, W], F32, name="acc%d%d%d" % (g, i, j))
            for n0 in range(0, W, NT):
                for h in range(PER):
                    for g in range(G):
                        rows = slice(g * ROWS, (g + 1) * ROWS)
                        nc.tensor.matmul_mx(
                            out=acc[(c, g, i, j)][:, h, n0 : n0 + NT],
                            lhsT=w_codes[i][rows, h * P : (h + 1) * P].bitcast(FP8X4),
                            lhsT_scale=w_scales[i][rows, h * P : (h + 1) * P],
                            rhs=x_codes[c][j][rows, n0 : n0 + NT].bitcast(FP8X4),
                            rhs_scale=x_scales[c][j][rows, n0 : n0 + NT],
                            start=True,
                            stop=True,
                        )

        def copy_z2(part):
            nc.scalar.copy(out=z2_t[part][:], in_=acc[part + (W2, X)][:])

        def step_q(part):
            nc.vector.scalar_tensor_tensor(
                out=q_t[part][:], in0=acc[part + (W1, X)][:], scalar=2.0, in1=d0_t[part][:],
                op0=ALU.mult, op1=ALU.subtract,
            )

        def step_e(part):
            for h in range(PER):
                nc.scalar.activation(
                    out=e_t[part][:, h, :], in_=q_t[part][:, h, :], func=EXP, scale=sh_t[:, part[1], h : h + 1]
                )

        def step_b(part):
            for h in range(PER):
                nc.vector.scalar_tensor_tensor(
                    out=b_t[part][:, h, :], in0=acc[part + (W1, DX)][:, h, :], scalar=k_t[:, part[1], h : h + 1],
                    in1=z2_t[part][:, h, :], op0=ALU.mult, op1=ALU.mult,
                )

        def step_c(part, features=range(PER)):
            for h in features:
                nc.vector.scalar_tensor_tensor(
                    out=c_t[part][:, h, :], in0=acc[part + (W2, DX)][:, h, :], scalar=og_t[:, part[1], h : h + 1],
                    in1=b_t[part][:, h, :], op0=ALU.mult, op1=ALU.add,
                )

        def step_f(engine, part, lo=0, hi=W):
            engine.tensor_tensor(
                out=f_t[part][:, :, lo:hi], in0=c_t[part][:, :, lo:hi], in1=e_t[part][:, :, lo:hi], op=ALU.mult
            )

        def step_y(engine, part):
            engine.tensor_tensor(out=y_t[part][:], in0=f_t[part][:], in1=base_t[part][:], op=ALU.add)

        def store_y(part):
            c, g = part
            nc.sync.dma_start(out=feature_rows(out_0[g * M : (g + 1) * M, :], c), in_=y_t[part][:])

        def round_y(part):
            nc.scalar.copy(
                out=yb_t[part][:].rearrange("q (a b h) -> q a h b", b=RUN, h=PER),
                in_=y_t[part][:].rearrange("q h (a b) -> q a h b", b=RUN),
            )

        def step_y_rounded(part, lo, hi):
            nc.vector.tensor_tensor(
                out=yb_t[part][:, lo * PER : hi * PER].rearrange("q (a b h) -> q a h b", b=RUN, h=PER),
                in0=f_t[part][:, :, lo:hi].rearrange("q h (a b) -> q a h b", b=RUN),
                in1=base_t[part][:, :, lo:hi].rearrange("q h (a b) -> q a h b", b=RUN),
                op=ALU.add,
            )

        def move_y(part, lo=0, hi=W):
            c, g = part
            nc.sync.dma_start(
                out=moved_t[c][g * ROWS : (g + 1) * ROWS, :, lo:hi], in_=yb_t[part][:].bitcast(F32)[:, lo:hi]
            )

        def pack_y(copy, c, lo=0, hi=W):
            copy(
                out=yq_t[c][:].bitcast(F32)[:, 2 * lo : 2 * hi].rearrange("p (a b r) -> p a r b", b=RUN, r=2),
                in_=moved_t[c][:, :, lo:hi].rearrange("p r (a b) -> p a r b", b=RUN),
            )

        def quant_y(c, lo=0, hi=W):
            at = slice(c * W + lo, c * W + hi)
            nc.vector.quantize_mx(
                out=y_codes[:, at].bitcast(FP8X4), scales=y_scales[:, at], in_=yq_t[c][:, PACK * lo : PACK * hi]
            )

        def store_words(c):
            nc.sync.dma_start(
                out=out_1[0].rearrange("p n u -> p (n u)").bitcast(I32)[:, cols(c)],
                in_=y_codes[:, cols(c)].bitcast(I32),
            )

        def store_scales(queue, quad):
            queue.dma_start(
                out=out_2[0, 4 * quad : 4 * quad + 4, :].bitcast(I32),
                in_=y_scales[QUAD * quad : QUAD * quad + 4, :].bitcast(I32),
            )

        first0, first1, last0, last1 = parts

        load_w(W2)
        load_x(0, X)
        for vec, vec_t in ((sh, sh_t), (og, og_t)):
            nc.scalar.dma_start(out=vec_t[:], in_=vec.rearrange("g (q h) o -> q g (h o)", h=PER))
        load_w(W1)
        load_x(0, DX)
        load_d0(first0)
        load_x(1, X)
        load_x(1, DX)
        load_d0(first1)
        load_d0(last0)
        load_base(first0)
        load_d0(last1)
        for part in (first1, last0, last1):
            load_base(part)

        round_w(W2)
        quant_w(W2)
        round_x(nc.vector.tensor_copy, 0, X)
        quant_x(0, X)
        product(0, W2, X)
        round_w(W1)
        nc.vector.scalar_tensor_tensor(out=k_t[:], in0=sh_t[:], scalar=2.0, in1=og_t[:], op0=ALU.mult, op1=ALU.mult)
        quant_w(W1)
        product(0, W1, X)
        round_x(nc.vector.tensor_copy, 0, DX, 0, NT)
        round_x(nc.scalar.copy, 0, DX, NT, W)
        copy_z2(first0)
        copy_z2(first1)
        quant_x(0, DX, 0, NT)
        quant_x(0, DX, NT, W)
        product(0, W1, DX)
        product(0, W2, DX)

        step_q(first0)
        round_x(nc.scalar.copy, 1, X)
        step_e(first0)
        step_b(first0)
        step_b(first1)
        step_c(first0, [0])
        quant_x(1, X)
        step_c(first0, [1])
        step_f(nc.gpsimd, first0)
        product(1, W2, X)
        round_x(nc.scalar.copy, 1, DX)
        step_c(first1)
        step_q(first1)
        product(1, W1, X)
        copy_z2(last0)
        step_e(first1)
        quant_x(1, DX)
        product(1, W1, DX)
        product(1, W2, DX)

        step_y(nc.vector, first0)
        store_y(first0)
        step_f(nc.gpsimd, first1)
        step_y(nc.gpsimd, first1)
        step_q(last0)
        copy_z2(last1)
        step_e(last0)
        round_y(first0)
        move_y(first0)
        step_q(last1)
        step_e(last1)
        step_b(last0)
        step_b(last1)
        round_y(first1)
        move_y(first1)
        step_c(last0)
        step_c(last1)

        halves = [(0, W // 2), (W // 2, W)]
        for lo, hi in halves:
            for part in (last0, last1):
                step_f(nc.vector, part, lo, hi)
            for part in (last0, last1):
                step_y_rounded(part, lo, hi)
                move_y(part, lo, hi)
        store_y(first1)
        for part in (last0, last1):
            step_y(nc.vector, part)
            store_y(part)
        pack_y(nc.vector.tensor_copy, 0)
        quant_y(0)
        store_words(0)
        for copy, (lo, hi) in zip((nc.scalar.copy, nc.vector.tensor_copy), halves):
            pack_y(copy, 1, lo, hi)
            quant_y(1, lo, hi)
        store_words(1)
        for quad in range(P // QUAD):
            store_scales((nc.scalar, nc.sync)[quad % 2], quad)
